import numpy as np
import ml_dtypes


def mxq(x, axis, fmt="e4m3"):
    dtype, down = {"e4m3": (ml_dtypes.float8_e4m3fn, 7), "e5m2": (ml_dtypes.float8_e5m2, 14)}[fmt]
    v = np.moveaxis(np.asarray(x, np.float32).astype(ml_dtypes.bfloat16).astype(np.float64), axis, -1)
    blocks = v.reshape(v.shape[:-1] + (-1, 32))
    amax = np.abs(blocks).max(-1, keepdims=True)
    byte = np.maximum(np.where(amax > 0, np.frexp(amax)[1] - 1 + 127, 0) - down, 1)
    scale = np.exp2(byte - 127.0)
    codes = (blocks / scale).astype(np.float32).astype(dtype).astype(np.float64)
    return np.moveaxis((codes * scale).reshape(v.shape), -1, axis)


WIDE = False


def mx_kscale(k):
    if not WIDE:
        return np.ones(k)
    levels = np.array([10, -10, 5, -5, 0])
    if k % 512:
        return np.exp2(np.random.permutation(np.resize(levels, k // 32))).repeat(32)
    a = np.empty((k // 512, 16))
    for p in range(k // 512):
        a[p, :8] = np.random.permutation(np.resize(levels, 8))
        for g in range(8):
            far = levels[np.abs(levels - a[p, g]) >= 10]
            a[p, g + 8] = far[np.random.randint(len(far))]
    return np.exp2(a.ravel()).repeat(32)


def f64(x):
    return np.asarray(x).astype(np.float64)


def striped8(idx):
    return np.asarray(idx).reshape(8, -1, 16).transpose(0, 2, 1).reshape(128, -1).astype(np.uint16)


def unstriped8(offs):
    return offs.reshape(8, 16, -1).transpose(0, 2, 1).reshape(8, -1).astype(np.int64)


def pick8(x, idx, run):
    r = np.arange(len(x))
    return x[r[:, None], idx[r % (8 * run) // run]]


E2M1 = np.array([0.0, 0.5, 1.0, 1.5, 2.0, 3.0, 4.0, 6.0, -0.0, -0.5, -1.0, -1.5, -2.0, -3.0, -4.0, -6.0])


def pack_weight(w, fmt):
    k, n = w.shape
    w = f64(np.asarray(w, np.float32).astype(ml_dtypes.bfloat16)).reshape(k // 32, 32, n)
    amax = np.abs(w).max(1)
    if fmt == "e4m3":
        byte = np.frexp(amax)[1] - 1 + 127 - 7
    else:
        mant, ex = np.frexp(amax / 6.0)
        byte = np.where(mant > 0.5, ex, ex - 1) + 127
    byte = np.clip(np.where(amax > 0, byte, 1), 1, 254)
    scaled = (w * np.exp2(127.0 - byte)[:, None, :]).reshape(k, n).astype(np.float32)
    by_word = np.ascontiguousarray(scaled.reshape(k // 512, 128, 4, n).transpose(0, 1, 3, 2))
    if fmt == "e4m3":
        words = by_word.astype(ml_dtypes.float8_e4m3fn).view(np.uint8)
    else:
        c = by_word.astype(ml_dtypes.float4_e2m1fn).view(np.uint8) & 0xF
        words = (c[..., 0::2] | (c[..., 1::2] << 4)).reshape(k // 512, 128, 2 * n)
    return np.ascontiguousarray(words), np.ascontiguousarray(byte.astype(np.uint8).reshape(k // 512, 16, n))


def unpack_weight(words, scales, fmt):
    g, _, n = scales.shape
    words = np.ascontiguousarray(words).reshape(g, 128, n, -1)
    if fmt == "e4m3":
        vals = words.view(ml_dtypes.float8_e4m3fn).astype(np.float64)
    else:
        nib = np.empty((g, 128, n, 4), np.uint8)
        nib[..., 0::2] = words & 0xF
        nib[..., 1::2] = words >> 4
        vals = E2M1[nib]
    vals = vals * np.repeat(np.exp2(scales.astype(np.float64) - 127.0), 8, axis=1)[..., None]
    return vals.transpose(0, 1, 3, 2).reshape(g * 512, n)


D, T, U, I, Q = 512, 1024, 1024, 512, 128


def setup_inputs():
    n = np.random.standard_normal
    idx = np.stack([np.random.permutation(T)[:I] for _ in range(8)])
    idx2 = np.stack([np.random.permutation(U)[:I] for _ in range(8)])
    idx3 = np.stack([np.random.permutation(T)[:I] for _ in range(8)])
    idx4 = np.stack([np.random.permutation(U)[:I] for _ in range(8)])
    idx5 = np.stack([np.random.permutation(U)[:I] for _ in range(8)])
    fd = mx_kscale(D)
    keysp = pack_weight(n((D, T)) / fd[:, None], "e2m1")
    notesp = pack_weight(n((D, U)) / fd[:, None], "e4m3")
    return {
        "query": (n((D, Q)) * 1.0 / np.sqrt(D) * fd[:, None]).astype(np.float32),
        "keys_words": keysp[0],
        "keys_scales": keysp[1],
        "notes_words": notesp[0],
        "notes_scales": notesp[1],
        "offs": striped8(idx),
        "offs2": striped8(idx2),
        "offs3": striped8(idx3),
        "offs4": striped8(idx4),
        "offs5": striped8(idx5),
    }


def reference(query, keys_words, keys_scales, notes_words, notes_scales, offs, offs2, offs3, offs4, offs5):
    idx = unstriped8(offs)
    idx2 = unstriped8(offs2)
    idx3 = unstriped8(offs3)
    idx4 = unstriped8(offs4)
    idx5 = unstriped8(offs5)
    keysu = unpack_weight(keys_words, keys_scales, "e2m1")
    notesu = unpack_weight(notes_words, notes_scales, "e4m3")
    queryq = mxq(f64(query), 0, "e4m3")
    a = queryq.T @ keysu
    b = queryq.T @ notesu
    f1 = np.zeros((Q, U))
    f1[np.arange(Q)[:, None], idx2[np.arange(Q) % 128 // 16]] = pick8(a, idx, 16)
    f2 = np.zeros((Q, U))
    f2[np.arange(Q)[:, None], idx4[np.arange(Q) % 128 // 16]] = pick8(a, idx3, 16)
    r = f1 - f2
    cc = b + r
    y = pick8(cc, idx5, 16)
    return y

@@ -1,0 +1,144 @@
+from contextlib import ExitStack
+
+import concourse.mybir as mybir
+
+D, T, U, SLOTS, Q = 512, 1024, 1024, 512, 128
+FLOPS = 2 * D * Q * (T + U)
+
+F32 = mybir.dt.float32
+BF16 = mybir.dt.bfloat16
+I32 = mybir.dt.int32
+U32 = mybir.dt.uint32
+U16 = mybir.dt.uint16
+U8 = mybir.dt.uint8
+FP8X4 = mybir.dt.float8_e4m3fn_x4
+FP4X4 = mybir.dt.float4_e2m1fn_x4
+COPY = mybir.ActivationFunctionType.Copy
+ADD = mybir.AluOpType.add
+SUB = mybir.AluOpType.subtract
+
+P = 128
+PACK = 4
+A_WIDTHS = (256, 256, 256, 128, 128)
+B_COLS = 512
+HALF = SLOTS // 2
+
+
+def load_plane(queue, plane, scales):
+    for quad in range(4):
+        queue.dma_start(
+            out=plane[32 * quad : 32 * quad + 4, :].bitcast(I32),
+            in_=scales[0, 4 * quad : 4 * quad + 4, :].bitcast(I32),
+        )
+
+
+def tile_attend_withdrawn_two_kernel(
+    tc, query, keys_words, keys_scales, notes_words, notes_scales, offs, offs2, offs3, offs4, offs5, out
+):
+    nc = tc.nc
+    with ExitStack() as ctx:
+        lists = ctx.enter_context(tc.tile_pool(name="lists", bufs=1))
+        keep = ctx.enter_context(tc.tile_pool(name="keep", bufs=1))
+        psum = ctx.enter_context(tc.psum_pool(name="psum", bufs=1))
+
+        k_plane = keep.tile([P, T], U8, align_bytes=64)
+        n_plane = keep.tile([P, U], U8, align_bytes=64)
+        f1 = keep.tile([P, U], F32)
+        f2 = keep.tile([P, U], F32)
+        nc.vector.memset(k_plane[:].bitcast(I32), 0)
+        nc.vector.memset(n_plane[:].bitcast(I32), 0)
+        nc.vector.memset(f1[:], 0.0)
+        nc.vector.memset(f2[:], 0.0)
+
+        q_raw = keep.tile([P, PACK, Q], F32)
+        nc.sync.dma_start(out=q_raw[:], in_=query.rearrange("(p j) w -> p j w", j=PACK))
+        k_words = keep.tile([P, 2 * T], U8, align_bytes=64)
+        nc.sync.dma_start(out=k_words[:].bitcast(I32), in_=keys_words[0].bitcast(I32))
+        load_plane(nc.sync, k_plane, keys_scales)
+
+        o1 = lists.tile([P, SLOTS // 16], U16, name="o1")
+        o2 = lists.tile([P, SLOTS // 16], U16, name="o2")
+        o3 = lists.tile([P, SLOTS // 16], U16, name="o3")
+        o4 = lists.tile([P, SLOTS // 16], U16, name="o4")
+        o5 = lists.tile([P, SLOTS // 16], U16, name="o5")
+        nc.sync.dma_start(o1[:], offs)
+        nc.sync.dma_start(o2[:], offs2)
+        nc.sync.dma_start(o3[:], offs3)
+        n_words = keep.tile([P, 4 * U], U8, align_bytes=64)
+        nc.sync.dma_start(
+            out=n_words[:].bitcast(I32), in_=notes_words[0].rearrange("p n t -> p (n t)").bitcast(I32)
+        )
+        load_plane(nc.sync, n_plane, notes_scales)
+        nc.sync.dma_start(o4[:], offs4)
+        nc.sync.dma_start(o5[:], offs5)
+
+        q_grouped = keep.tile([P, Q, PACK], BF16, align_bytes=64)
+        nc.vector.tensor_copy(
+            out=q_grouped[:].rearrange("p (c i) j -> p c j i", i=4),
+            in_=q_raw[:].rearrange("p j (c i) -> p c j i", i=4),
+        )
+        q_codes = keep.tile([P, Q], U32, align_bytes=64)
+        q_plane = keep.tile([P, Q], U8, align_bytes=64)
+        nc.vector.quantize_mx(
+            out=q_codes[:].bitcast(FP8X4), scales=q_plane[:], in_=q_grouped[:].rearrange("p w j -> p (w j)")
+        )
+
+        a = keep.tile([P, T], F32)
+        for c, width in enumerate(A_WIDTHS):
+            first = sum(A_WIDTHS[:c])
+            cols = slice(first, first + width)
+            bank = psum.tile([P, width], F32, name=f"a_bank{c}")
+            nc.tensor.matmul_mx(
+                out=bank[:],
+                lhsT=q_codes[:].bitcast(FP8X4),
+                lhsT_scale=q_plane[:],
+                rhs=k_words[:, 2 * first : 2 * (first + width)].bitcast(FP4X4),
+                rhs_scale=k_plane[:, cols],
+                start=True,
+                stop=True,
+            )
+            if c in (0, 2):
+                nc.scalar.activation(a[:, cols], bank[:], COPY)
+            else:
+                nc.vector.tensor_copy(a[:, cols], bank[:])
+
+        b_banks = []
+        for c in range(U // B_COLS):
+            cols = slice(c * B_COLS, (c + 1) * B_COLS)
+            bank = psum.tile([P, B_COLS], F32, name=f"b_bank{c}")
+            nc.tensor.matmul_mx(
+                out=bank[:],
+                lhsT=q_codes[:].bitcast(FP8X4),
+                lhsT_scale=q_plane[:],
+                rhs=n_words[:, 4 * c * B_COLS : 4 * (c + 1) * B_COLS].bitcast(FP8X4),
+                rhs_scale=n_plane[:, cols],
+                start=True,
+                stop=True,
+            )
+            b_banks.append(bank)
+
+        given_lo = keep.tile([P, HALF], F32)
+        given_hi = keep.tile([P, HALF], F32)
+        taken = keep.tile([P, SLOTS], F32)
+        lo, hi = slice(0, HALF // 16), slice(HALF // 16, SLOTS // 16)
+        nc.scalar.activation(given_lo[:], a[:].indirect(o1[:, lo]), COPY)
+        nc.vector.tensor_copy(given_hi[:], a[:].indirect(o1[:, hi]))
+        nc.scalar.activation(taken[:], a[:].indirect(o3[:]), COPY)
+        nc.vector.tensor_copy(f1[:].indirect(o2[:, lo]), given_lo[:])
+        nc.vector.tensor_copy(f1[:].indirect(o2[:, hi]), given_hi[:])
+        nc.vector.tensor_copy(f2[:].indirect(o4[:]), taken[:])
+
+        b = keep.tile([P, U], F32)
+        for c in range(U // B_COLS):
+            nc.scalar.activation(b[:, c * B_COLS : (c + 1) * B_COLS], b_banks[c][:], COPY)
+        b_f1 = keep.tile([P, U], F32)
+        nc.gpsimd.tensor_tensor(b_f1[:], b[:], f1[:], ADD)
+        cc = keep.tile([P, U], F32)
+        nc.vector.tensor_tensor(cc[:], b_f1[:], f2[:], SUB)
+
+        y_lo = keep.tile([P, HALF], F32)
+        y_hi = keep.tile([P, HALF], F32)
+        nc.scalar.activation(y_lo[:], cc[:].indirect(o5[:, lo]), COPY)
+        nc.vector.tensor_copy(y_hi[:], cc[:].indirect(o5[:, hi]))
+        nc.scalar.dma_start(out=out[:, 0:HALF], in_=y_lo[:])
+        nc.sync.dma_start(out=out[:, HALF:SLOTS], in_=y_hi[:])

@@ -16,12 +16,14 @@ FP4X4 = mybir.dt.float4_e2m1fn_x4
 COPY = mybir.ActivationFunctionType.Copy
 ADD = mybir.AluOpType.add
 SUB = mybir.AluOpType.subtract
+MULT = mybir.AluOpType.mult
 
 P = 128
 PACK = 4
 A_WIDTHS = (256, 256, 256, 128, 128)
 B_COLS = 512
 HALF = SLOTS // 2
+FIRST = 128
 
 
 def load_plane(queue, plane, scales):
@@ -44,11 +46,11 @@ def tile_attend_withdrawn_two_kernel(
         k_plane = keep.tile([P, T], U8, align_bytes=64)
         n_plane = keep.tile([P, U], U8, align_bytes=64)
         f1 = keep.tile([P, U], F32)
-        f2 = keep.tile([P, U], F32)
         nc.vector.memset(k_plane[:].bitcast(I32), 0)
         nc.vector.memset(n_plane[:].bitcast(I32), 0)
         nc.vector.memset(f1[:], 0.0)
-        nc.vector.memset(f2[:], 0.0)
+        ones = keep.tile([P, FIRST], F32)
+        nc.vector.memset(ones[:], 1.0)
 
         q_raw = keep.tile([P, PACK, Q], F32)
         nc.sync.dma_start(out=q_raw[:], in_=query.rearrange("(p j) w -> p j w", j=PACK))
@@ -72,17 +74,24 @@ def tile_attend_withdrawn_two_kernel(
         nc.sync.dma_start(o4[:], offs4)
         nc.sync.dma_start(o5[:], offs5)
 
-        q_grouped = keep.tile([P, Q, PACK], BF16, align_bytes=64)
-        nc.vector.tensor_copy(
-            out=q_grouped[:].rearrange("p (c i) j -> p c j i", i=4),
-            in_=q_raw[:].rearrange("p j (c i) -> p c j i", i=4),
-        )
+        q_grouped = keep.tile([P, Q, PACK], BF16, align_bytes=64, tag="shared")
         q_codes = keep.tile([P, Q], U32, align_bytes=64)
         q_plane = keep.tile([P, Q], U8, align_bytes=64)
-        nc.vector.quantize_mx(
-            out=q_codes[:].bitcast(FP8X4), scales=q_plane[:], in_=q_grouped[:].rearrange("p w j -> p (w j)")
-        )
+        q_halves = (slice(0, Q // 2), slice(Q // 2, Q))
+        for rows in q_halves:
+            nc.vector.tensor_copy(
+                out=q_grouped[:, rows, :].rearrange("p (c i) j -> p c j i", i=4),
+                in_=q_raw[:, :, rows].rearrange("p j (c i) -> p c j i", i=4),
+            )
+        for rows in q_halves:
+            nc.vector.quantize_mx(
+                out=q_codes[:, rows].bitcast(FP8X4),
+                scales=q_plane[:, rows],
+                in_=q_grouped[:, rows, :].rearrange("p w j -> p (w j)"),
+            )
 
+        f2 = keep.tile([P, U], F32, align_bytes=64, tag="shared")
+        nc.gpsimd.memset(f2[:], 0.0)
         a = keep.tile([P, T], F32)
         for c, width in enumerate(A_WIDTHS):
             first = sum(A_WIDTHS[:c])
@@ -117,15 +126,16 @@ def tile_attend_withdrawn_two_kernel(
             )
             b_banks.append(bank)
 
-        given_lo = keep.tile([P, HALF], F32)
-        given_hi = keep.tile([P, HALF], F32)
+        given_first = keep.tile([P, FIRST], F32)
+        given_rest = keep.tile([P, SLOTS - FIRST], F32)
+        head, rest = slice(0, FIRST // 16), slice(FIRST // 16, SLOTS // 16)
         taken = keep.tile([P, SLOTS], F32)
         lo, hi = slice(0, HALF // 16), slice(HALF // 16, SLOTS // 16)
-        nc.scalar.activation(given_lo[:], a[:].indirect(o1[:, lo]), COPY)
-        nc.vector.tensor_copy(given_hi[:], a[:].indirect(o1[:, hi]))
+        nc.vector.tensor_tensor(given_first[:], a[:].indirect(o1[:, head]), ones[:], MULT)
+        nc.scalar.activation(given_rest[:], a[:].indirect(o1[:, rest]), COPY)
         nc.scalar.activation(taken[:], a[:].indirect(o3[:]), COPY)
-        nc.vector.tensor_copy(f1[:].indirect(o2[:, lo]), given_lo[:])
-        nc.vector.tensor_copy(f1[:].indirect(o2[:, hi]), given_hi[:])
+        nc.vector.tensor_copy(f1[:].indirect(o2[:, head]), given_first[:])
+        nc.vector.tensor_copy(f1[:].indirect(o2[:, rest]), given_rest[:])
         nc.vector.tensor_copy(f2[:].indirect(o4[:]), taken[:])
 
         b = keep.tile([P, U], F32)

@@ -1,6 +1,7 @@
 from contextlib import ExitStack
 
 import concourse.mybir as mybir
+from concourse.masks import make_identity
 
 D, T, U, SLOTS, Q = 512, 1024, 1024, 512, 128
 FLOPS = 2 * D * Q * (T + U)
@@ -24,6 +25,7 @@ A_WIDTHS = (256, 256, 256, 128, 128)
 B_COLS = 512
 HALF = SLOTS // 2
 FIRST = 128
+TURNED = 768
 
 
 def load_plane(queue, plane, scales):
@@ -47,6 +49,9 @@ def tile_attend_withdrawn_two_kernel(
         n_plane = keep.tile([P, U], U8, align_bytes=64)
         f1 = keep.tile([P, U], F32)
         nc.vector.memset(k_plane[:].bitcast(I32), 0)
+        ident = keep.tile([P, P], F32)
+        nc.vector.memset(ident[:], 0.0)
+        make_identity(nc, ident[:], nomemset=True)
         nc.vector.memset(n_plane[:].bitcast(I32), 0)
         nc.vector.memset(f1[:], 0.0)
         ones = keep.tile([P, FIRST], F32)
@@ -96,7 +101,7 @@ def tile_attend_withdrawn_two_kernel(
         for c, width in enumerate(A_WIDTHS):
             first = sum(A_WIDTHS[:c])
             cols = slice(first, first + width)
-            bank = psum.tile([P, width], F32, name=f"a_bank{c}")
+            bank = psum.tile([P, width], F32, name=f"a_bank{c}", tag=f"first{c}")
             nc.tensor.matmul_mx(
                 out=bank[:],
                 lhsT=q_codes[:].bitcast(FP8X4),
@@ -114,7 +119,7 @@ def tile_attend_withdrawn_two_kernel(
         b_banks = []
         for c in range(U // B_COLS):
             cols = slice(c * B_COLS, (c + 1) * B_COLS)
-            bank = psum.tile([P, B_COLS], F32, name=f"b_bank{c}")
+            bank = psum.tile([P, B_COLS], F32, name=f"b_bank{c}", tag=f"second{c}")
             nc.tensor.matmul_mx(
                 out=bank[:],
                 lhsT=q_codes[:].bitcast(FP8X4),
@@ -141,10 +146,43 @@ def tile_attend_withdrawn_two_kernel(
         b = keep.tile([P, U], F32)
         for c in range(U // B_COLS):
             nc.scalar.activation(b[:, c * B_COLS : (c + 1) * B_COLS], b_banks[c][:], COPY)
-        b_f1 = keep.tile([P, U], F32)
-        nc.gpsimd.tensor_tensor(b_f1[:], b[:], f1[:], ADD)
         cc = keep.tile([P, U], F32)
-        nc.vector.tensor_tensor(cc[:], b_f1[:], f2[:], SUB)
+        tail = slice(TURNED, U)
+        b_f1 = keep.tile([P, U - TURNED], F32)
+        nc.gpsimd.tensor_tensor(b_f1[:], b[:, tail], f1[:, tail], ADD)
+        nc.gpsimd.tensor_tensor(cc[:, tail], b_f1[:], f2[:, tail], SUB)
+
+        pairs = TURNED // (2 * P)
+        turned_banks = []
+        for c in range(pairs):
+            bank = psum.tile([P, 2 * P], F32, name=f"turned_bank{c}", tag=f"first{c}")
+            for h in range(2):
+                blk = slice((2 * c + h) * P, (2 * c + h + 1) * P)
+                nc.tensor.matmul(
+                    bank[:, h * P : (h + 1) * P], lhsT=b[:, blk], rhs=ident[:], is_transpose=True,
+                    start=(h == 0), stop=False,
+                )
+            turned_banks.append(bank)
+        turned = []
+        for c in range(pairs):
+            for h in range(2):
+                blk = slice((2 * c + h) * P, (2 * c + h + 1) * P)
+                nc.tensor.matmul(
+                    turned_banks[c][:, h * P : (h + 1) * P], lhsT=f1[:, blk], rhs=ident[:], is_transpose=True,
+                    start=False, stop=(h == 1),
+                )
+            piece = keep.tile([P, 2 * P], F32, name=f"turned{c}")
+            nc.scalar.activation(piece[:], turned_banks[c][:], COPY)
+            turned.append(piece)
+        for c, first in enumerate(range(0, TURNED, B_COLS)):
+            width = min(B_COLS, TURNED - first)
+            cols = slice(first, first + width)
+            bank = psum.tile([P, width], F32, name=f"sum_bank{c}", tag=f"second{c}")
+            for h in range(width // P):
+                nc.tensor.transpose(
+                    bank[:, h * P : (h + 1) * P], turned[2 * c + h // 2][:, (h % 2) * P : (h % 2 + 1) * P], ident[:]
+                )
+            nc.vector.tensor_tensor(cc[:, cols], bank[:], f2[:, cols], SUB)
 
         y_lo = keep.tile([P, HALF], F32)
         y_hi = keep.tile([P, HALF], F32)

from contextlib import ExitStack

import concourse.mybir as mybir
from concourse.masks import make_identity

D, T, U, SLOTS, Q = 512, 1024, 1024, 512, 128
FLOPS = 2 * D * Q * (T + U)

F32 = mybir.dt.float32
BF16 = mybir.dt.bfloat16
I32 = mybir.dt.int32
U32 = mybir.dt.uint32
U16 = mybir.dt.uint16
U8 = mybir.dt.uint8
FP8X4 = mybir.dt.float8_e4m3fn_x4
FP4X4 = mybir.dt.float4_e2m1fn_x4
COPY = mybir.ActivationFunctionType.Copy
ADD = mybir.AluOpType.add
SUB = mybir.AluOpType.subtract
MULT = mybir.AluOpType.mult

P = 128
PACK = 4
A_WIDTHS = (256, 256, 256, 128, 128)
B_COLS = 512
HALF = SLOTS // 2
FIRST = 128
TURNED = 768


def load_plane(queue, plane, scales):
    for quad in range(4):
        queue.dma_start(
            out=plane[32 * quad : 32 * quad + 4, :].bitcast(I32),
            in_=scales[0, 4 * quad : 4 * quad + 4, :].bitcast(I32),
        )


def tile_attend_withdrawn_two_kernel(
    tc, query, keys_words, keys_scales, notes_words, notes_scales, offs, offs2, offs3, offs4, offs5, out
):
    nc = tc.nc
    with ExitStack() as ctx:
        lists = ctx.enter_context(tc.tile_pool(name="lists", bufs=1))
        keep = ctx.enter_context(tc.tile_pool(name="keep", bufs=1))
        psum = ctx.enter_context(tc.psum_pool(name="psum", bufs=1))

        k_plane = keep.tile([P, T], U8, align_bytes=64)
        n_plane = keep.tile([P, U], U8, align_bytes=64)
        f1 = keep.tile([P, U], F32)
        nc.vector.memset(k_plane[:].bitcast(I32), 0)
        ident = keep.tile([P, P], F32)
        nc.vector.memset(ident[:], 0.0)
        make_identity(nc, ident[:], nomemset=True)
        nc.vector.memset(n_plane[:].bitcast(I32), 0)
        nc.vector.memset(f1[:], 0.0)
        ones = keep.tile([P, FIRST], F32)
        nc.vector.memset(ones[:], 1.0)

        q_raw = keep.tile([P, PACK, Q], F32)
        nc.sync.dma_start(out=q_raw[:], in_=query.rearrange("(p j) w -> p j w", j=PACK))
        k_words = keep.tile([P, 2 * T], U8, align_bytes=64)
        nc.sync.dma_start(out=k_words[:].bitcast(I32), in_=keys_words[0].bitcast(I32))
        load_plane(nc.sync, k_plane, keys_scales)

        o1 = lists.tile([P, SLOTS // 16], U16, name="o1")
        o2 = lists.tile([P, SLOTS // 16], U16, name="o2")
        o3 = lists.tile([P, SLOTS // 16], U16, name="o3")
        o4 = lists.tile([P, SLOTS // 16], U16, name="o4")
        o5 = lists.tile([P, SLOTS // 16], U16, name="o5")
        nc.sync.dma_start(o1[:], offs)
        nc.sync.dma_start(o2[:], offs2)
        nc.sync.dma_start(o3[:], offs3)
        n_words = keep.tile([P, 4 * U], U8, align_bytes=64)
        nc.sync.dma_start(
            out=n_words[:].bitcast(I32), in_=notes_words[0].rearrange("p n t -> p (n t)").bitcast(I32)
        )
        load_plane(nc.sync, n_plane, notes_scales)
        nc.sync.dma_start(o4[:], offs4)
        nc.sync.dma_start(o5[:], offs5)

        q_grouped = keep.tile([P, Q, PACK], BF16, align_bytes=64, tag="shared")
        q_codes = keep.tile([P, Q], U32, align_bytes=64)
        q_plane = keep.tile([P, Q], U8, align_bytes=64)
        q_halves = (slice(0, Q // 2), slice(Q // 2, Q))
        for rows in q_halves:
            nc.vector.tensor_copy(
                out=q_grouped[:, rows, :].rearrange("p (c i) j -> p c j i", i=4),
                in_=q_raw[:, :, rows].rearrange("p j (c i) -> p c j i", i=4),
            )
        for rows in q_halves:
            nc.vector.quantize_mx(
                out=q_codes[:, rows].bitcast(FP8X4),
                scales=q_plane[:, rows],
                in_=q_grouped[:, rows, :].rearrange("p w j -> p (w j)"),
            )

        f2 = keep.tile([P, U], F32, align_bytes=64, tag="shared")
        nc.gpsimd.memset(f2[:], 0.0)
        a = keep.tile([P, T], F32)
        for c, width in enumerate(A_WIDTHS):
            first = sum(A_WIDTHS[:c])
            cols = slice(first, first + width)
            bank = psum.tile([P, width], F32, name=f"a_bank{c}", tag=f"first{c}")
            nc.tensor.matmul_mx(
                out=bank[:],
                lhsT=q_codes[:].bitcast(FP8X4),
                lhsT_scale=q_plane[:],
                rhs=k_words[:, 2 * first : 2 * (first + width)].bitcast(FP4X4),
                rhs_scale=k_plane[:, cols],
                start=True,
                stop=True,
            )
            if c in (0, 2):
                nc.scalar.activation(a[:, cols], bank[:], COPY)
            else:
                nc.vector.tensor_copy(a[:, cols], bank[:])

        b_banks = []
        for c in range(U // B_COLS):
            cols = slice(c * B_COLS, (c + 1) * B_COLS)
            bank = psum.tile([P, B_COLS], F32, name=f"b_bank{c}", tag=f"second{c}")
            nc.tensor.matmul_mx(
                out=bank[:],
                lhsT=q_codes[:].bitcast(FP8X4),
                lhsT_scale=q_plane[:],
                rhs=n_words[:, 4 * c * B_COLS : 4 * (c + 1) * B_COLS].bitcast(FP8X4),
                rhs_scale=n_plane[:, cols],
                start=True,
                stop=True,
            )
            b_banks.append(bank)

        given_first = keep.tile([P, FIRST], F32)
        given_rest = keep.tile([P, SLOTS - FIRST], F32)
        head, rest = slice(0, FIRST // 16), slice(FIRST // 16, SLOTS // 16)
        taken = keep.tile([P, SLOTS], F32)
        lo, hi = slice(0, HALF // 16), slice(HALF // 16, SLOTS // 16)
        nc.vector.tensor_tensor(given_first[:], a[:].indirect(o1[:, head]), ones[:], MULT)
        nc.scalar.activation(given_rest[:], a[:].indirect(o1[:, rest]), COPY)
        nc.scalar.activation(taken[:], a[:].indirect(o3[:]), COPY)
        nc.vector.tensor_copy(f1[:].indirect(o2[:, head]), given_first[:])
        nc.vector.tensor_copy(f1[:].indirect(o2[:, rest]), given_rest[:])
        nc.vector.tensor_copy(f2[:].indirect(o4[:]), taken[:])

        b = keep.tile([P, U], F32)
        for c in range(U // B_COLS):
            nc.scalar.activation(b[:, c * B_COLS : (c + 1) * B_COLS], b_banks[c][:], COPY)
        cc = keep.tile([P, U], F32)
        tail = slice(TURNED, U)
        b_f1 = keep.tile([P, U - TURNED], F32)
        nc.gpsimd.tensor_tensor(b_f1[:], b[:, tail], f1[:, tail], ADD)
        nc.gpsimd.tensor_tensor(cc[:, tail], b_f1[:], f2[:, tail], SUB)

        pairs = TURNED // (2 * P)
        turned_banks = []
        for c in range(pairs):
            bank = psum.tile([P, 2 * P], F32, name=f"turned_bank{c}", tag=f"first{c}")
            for h in range(2):
                blk = slice((2 * c + h) * P, (2 * c + h + 1) * P)
                nc.tensor.matmul(
                    bank[:, h * P : (h + 1) * P], lhsT=b[:, blk], rhs=ident[:], is_transpose=True,
                    start=(h == 0), stop=False,
                )
            turned_banks.append(bank)
        turned = []
        for c in range(pairs):
            for h in range(2):
                blk = slice((2 * c + h) * P, (2 * c + h + 1) * P)
                nc.tensor.matmul(
                    turned_banks[c][:, h * P : (h + 1) * P], lhsT=f1[:, blk], rhs=ident[:], is_transpose=True,
                    start=False, stop=(h == 1),
                )
            piece = keep.tile([P, 2 * P], F32, name=f"turned{c}")
            nc.scalar.activation(piece[:], turned_banks[c][:], COPY)
            turned.append(piece)
        for c, first in enumerate(range(0, TURNED, B_COLS)):
            width = min(B_COLS, TURNED - first)
            cols = slice(first, first + width)
            bank = psum.tile([P, width], F32, name=f"sum_bank{c}", tag=f"second{c}")
            for h in range(width // P):
                nc.tensor.transpose(
                    bank[:, h * P : (h + 1) * P], turned[2 * c + h // 2][:, (h % 2) * P : (h % 2 + 1) * P], ident[:]
                )
            nc.vector.tensor_tensor(cc[:, cols], bank[:], f2[:, cols], SUB)

        y_lo = keep.tile([P, HALF], F32)
        y_hi = keep.tile([P, HALF], F32)
        nc.scalar.activation(y_lo[:], cc[:].indirect(o5[:, lo]), COPY)
        nc.vector.tensor_copy(y_hi[:], cc[:].indirect(o5[:, hi]))
        nc.scalar.dma_start(out=out[:, 0:HALF], in_=y_lo[:])
        nc.sync.dma_start(out=out[:, HALF:SLOTS], in_=y_hi[:])
